import numpy as np
import ml_dtypes


def mxq(x, axis, fmt="e4m3"):
    dtype, down = {"e4m3": (ml_dtypes.float8_e4m3fn, 7), "e5m2": (ml_dtypes.float8_e5m2, 14)}[fmt]
    v = np.moveaxis(np.asarray(x, np.float32).astype(ml_dtypes.bfloat16).astype(np.float64), axis, -1)
    blocks = v.reshape(v.shape[:-1] + (-1, 32))
    amax = np.abs(blocks).max(-1, keepdims=True)
    byte = np.maximum(np.where(amax > 0, np.frexp(amax)[1] - 1 + 127, 0) - down, 1)
    scale = np.exp2(byte - 127.0)
    codes = (blocks / scale).astype(np.float32).astype(dtype).astype(np.float64)
    return np.moveaxis((codes * scale).reshape(v.shape), -1, axis)


WIDE = False


def mx_kscale(k):
    if not WIDE:
        return np.ones(k)
    levels = np.array([10, -10, 5, -5, 0])
    if k % 512:
        return np.exp2(np.random.permutation(np.resize(levels, k // 32))).repeat(32)
    a = np.empty((k // 512, 16))
    for p in range(k // 512):
        a[p, :8] = np.random.permutation(np.resize(levels, 8))
        for g in range(8):
            far = levels[np.abs(levels - a[p, g]) >= 10]
            a[p, g + 8] = far[np.random.randint(len(far))]
    return np.exp2(a.ravel()).repeat(32)


BF16 = ml_dtypes.bfloat16


def bf(x):
    return np.asarray(x, np.float32).astype(BF16)


def f64(x):
    return np.asarray(x).astype(np.float64)


E2M1 = np.array([0.0, 0.5, 1.0, 1.5, 2.0, 3.0, 4.0, 6.0, -0.0, -0.5, -1.0, -1.5, -2.0, -3.0, -4.0, -6.0])


def pack_weight(w, fmt):
    k, n = w.shape
    w = f64(bf(w)).reshape(k // 32, 32, n)
    amax = np.abs(w).max(1)
    if fmt == "e4m3":
        byte = np.frexp(amax)[1] - 1 + 127 - 7
    else:
        mant, ex = np.frexp(amax / 6.0)
        byte = np.where(mant > 0.5, ex, ex - 1) + 127
    byte = np.clip(np.where(amax > 0, byte, 1), 1, 254)
    scaled = (w * np.exp2(127.0 - byte)[:, None, :]).reshape(k, n).astype(np.float32)
    by_word = np.ascontiguousarray(scaled.reshape(k // 512, 128, 4, n).transpose(0, 1, 3, 2))
    if fmt == "e4m3":
        words = by_word.astype(ml_dtypes.float8_e4m3fn).view(np.uint8)
    else:
        c = by_word.astype(ml_dtypes.float4_e2m1fn).view(np.uint8) & 0xF
        words = c[..., 0::2] | (c[..., 1::2] << 4)
    return np.ascontiguousarray(words), np.ascontiguousarray(byte.astype(np.uint8).reshape(k // 512, 16, n))


def unpack_weight(words, scales, fmt):
    g, p, n, _ = words.shape
    if fmt == "e4m3":
        vals = np.ascontiguousarray(words).view(ml_dtypes.float8_e4m3fn).astype(np.float64)
    else:
        nib = np.empty((g, p, n, 4), np.uint8)
        nib[..., 0::2] = words & 0xF
        nib[..., 1::2] = words >> 4
        vals = E2M1[nib]
    vals = vals * np.repeat(np.exp2(scales.astype(np.float64) - 127.0), 8, axis=1)[..., None]
    return vals.transpose(0, 1, 3, 2).reshape(g * 512, n)
def pack4(w):
    words, scales = pack_weight(w, "e2m1")
    return words.reshape(words.shape[0], 128, -1), scales


def unpack4(words, scales):
    return unpack_weight(words.reshape(words.shape[0], 128, -1, 2), scales, "e2m1")


def planes(Y):
    n, m = Y.shape
    b = f64(bf(Y)).reshape(n // 32, 32, m)
    amax = np.abs(b).max(1)
    byte = np.clip(np.where(amax > 0, np.frexp(amax)[1] - 1 + 127 - 7, 1), 1, 254)
    codes = (b * np.exp2(127.0 - byte)[:, None, :]).reshape(n, m).astype(np.float32).astype(ml_dtypes.float8_e4m3fn).view(np.uint8)
    words = codes.reshape(n // 512, 128, 4, m).transpose(0, 1, 3, 2)
    return np.ascontiguousarray(words), np.ascontiguousarray(byte.astype(np.uint8).reshape(n // 512, 16, m))


G, R, NX, NU, NP = 4, 512, 512, 1024, 1024

def setup_inputs():
    s = mx_kscale(NX)
    t = np.stack([mx_kscale(NU) for i in range(G)])
    x0 = np.random.randn(R, NX) * s
    gain = np.random.randn(G, NX, NU) / np.sqrt(NX) * t[:, None, :] / s[None, :, None]
    free = np.random.randn(G, NX, NP) / np.sqrt(NX) / s[None, :, None]
    forced = 1.3 * np.random.randn(G, NU, NP) / np.sqrt(NU) / t[:, :, None]
    gain_words, gain_scales = pack4(gain.reshape(G * NX, NU))
    free_words, free_scales = pack4(free.reshape(G * NX, NP))
    forced_words, forced_scales = pack4(forced.reshape(G * NU, NP))
    u_max = 0.8 * np.exp(0.3 * np.random.randn(G, NU)) * t
    u_min = -0.8 * np.exp(0.3 * np.random.randn(G, NU)) * t
    return {"x0": bf(x0), "gain_words": gain_words, "gain_scales": gain_scales,
            "free_words": free_words, "free_scales": free_scales,
            "forced_words": forced_words, "forced_scales": forced_scales,
            "u_max": bf(u_max), "u_min": bf(u_min),
            "ref": bf(np.random.randn(R, NP)),
            "w": bf(np.exp(0.8 * np.random.randn(G, NP)))}

def reference(x0, gain_words, gain_scales, free_words, free_scales, forced_words, forced_scales, u_max, u_min, ref, w):
    gain = unpack4(gain_words, gain_scales).reshape(G, NX, NU)
    free = unpack4(free_words, free_scales).reshape(G, NX, NP)
    forced = unpack4(forced_words, forced_scales).reshape(G, NU, NP)
    xq = mxq(f64(x0), 1, "e4m3")
    u = xq @ gain
    u = np.maximum(np.minimum(u, f64(u_max)[:, None, :]), f64(u_min)[:, None, :])
    uq = mxq(u, 2, "e4m3")
    pred = (xq @ free) + (uq @ forced)
    y = (pred - f64(ref)[None, :, :]) * f64(w)[:, None, :]
    Y = y.reshape(G * R, NP).T
    words, scales = planes(Y)
    return y, words, scales

@@ -1,0 +1,321 @@
+from contextlib import ExitStack
+
+import concourse.mybir as mybir
+from concourse.masks import make_identity
+
+G, R, NX, NU, NP = 4, 512, 512, 1024, 1024
+FLOPS = 2 * G * R * (NX * NU + NX * NP + NU * NP)
+
+F32 = mybir.dt.float32
+BF16 = mybir.dt.bfloat16
+I32 = mybir.dt.int32
+U32 = mybir.dt.uint32
+U8 = mybir.dt.uint8
+FP8X4 = mybir.dt.float8_e4m3fn_x4
+FP4X4 = mybir.dt.float4_e2m1fn_x4
+ALU = mybir.AluOpType
+
+P = 128
+BANK = 512
+TILES = R // P
+UNITS = G * TILES
+
+
+def tile_condensed_mpc_tracking_error_k7_kernel(
+    tc, x0, gain_words, gain_scales, free_words, free_scales, forced_words, forced_scales,
+    u_max, u_min, ref, w, out_0, out_1, out_2,
+):
+    nc = tc.nc
+    with ExitStack() as ctx:
+        keep = ctx.enter_context(tc.tile_pool(name="keep", bufs=1))
+        work = ctx.enter_context(tc.tile_pool(name="work", bufs=2))
+        psum = ctx.enter_context(tc.psum_pool(name="psum", bufs=1))
+        ctx.enter_context(tc.manual_schedule())
+
+        ident = keep.tile([P, P], F32, name="ident")
+        make_identity(nc, ident[:])
+
+        gain_sc = keep.tile([P, G, NU], U8, name="gain_sc", align_bytes=64)
+        free_sc = keep.tile([P, G, NP], U8, name="free_sc", align_bytes=64)
+        forced_sc = keep.tile([P, 2 * G, NP], U8, name="forced_sc", align_bytes=64)
+        limit_rows = keep.tile([P, BANK], BF16, name="limit_rows")
+        nc.vector.memset(gain_sc[:].bitcast(I32), 0)
+        nc.vector.memset(limit_rows[:].bitcast(F32), 0.0)
+        nc.vector.memset(free_sc[:].bitcast(I32), 0)
+        nc.vector.memset(forced_sc[:].bitcast(I32), 0)
+
+        def load_scales(plane, rows):
+            by_row = rows.rearrange("g (q r) n -> r q g n", r=4)
+            for r in range(4):
+                nc.sync.dma_start(out=plane[r:P:32, :, :].bitcast(I32), in_=by_row[r].bitcast(I32))
+
+        gain_w, free_w, forced_w, w_rows, ref_rows = {}, {}, {}, {}, {}
+
+        def load_gain(g):
+            gain_w[g] = keep.tile([P, 2 * NU], U8, name="gain_w%d" % g, align_bytes=64)
+            nc.sync.dma_start(out=gain_w[g][:].bitcast(I32), in_=gain_words[g].bitcast(I32))
+
+        def load_responses(g):
+            free_w[g] = keep.tile([P, 2 * NP], U8, name="free_w%d" % g, align_bytes=64)
+            nc.sync.dma_start(out=free_w[g][:].bitcast(I32), in_=free_words[g].bitcast(I32))
+            forced_w[g] = keep.tile([P, 2, 2 * NP], U8, name="forced_w%d" % g, align_bytes=64)
+            nc.sync.dma_start(
+                out=forced_w[g][:].bitcast(I32),
+                in_=forced_words[2 * g : 2 * g + 2].rearrange("h p n -> p h n").bitcast(I32),
+            )
+
+        def load_w(g):
+            w_rows[g] = keep.tile([P, NP], BF16, name="w_rows%d" % g)
+            nc.sync.dma_start(out=w_rows[g][:], in_=w[g].partition_broadcast(P))
+
+        def load_ref(j):
+            ref_rows[j] = keep.tile([P, NP], BF16, name="ref_rows%d" % j)
+            nc.sync.dma_start(out=ref_rows[j][:], in_=ref[j * P : (j + 1) * P, :])
+
+        x_first = keep.tile([P, NX], BF16, name="x_first")
+        x_rest = keep.tile([P, TILES - 1, NX], BF16, name="x_rest")
+        nc.sync.dma_start(out=x_first[:], in_=x0[0:P, :])
+        load_gain(0)
+        load_scales(gain_sc, gain_scales)
+        nc.sync.dma_start(out=x_rest[:], in_=x0[P:R, :].rearrange("(j p) k -> p j k", p=P))
+        nc.sync.dma_start(out=limit_rows[0:8, :], in_=u_max.rearrange("g (h k) -> (g h) k", h=2))
+        nc.sync.dma_start(out=limit_rows[8:16, :], in_=u_min.rearrange("g (h k) -> (g h) k", h=2))
+        load_scales(free_sc, free_scales)
+        load_scales(forced_sc, forced_scales)
+        load_responses(0)
+        load_ref(0)
+        load_w(0)
+        load_ref(1)
+        load_gain(1)
+        load_ref(2)
+        load_ref(3)
+        load_responses(1)
+        load_w(1)
+
+        x_codes, x_sc, x_bank, x_bf = {}, {}, {}, {}
+
+        def turn_x(j):
+            rows = x_first[:] if j == 0 else x_rest[:, j - 1, :]
+            words = rows.bitcast(F32)
+            x_bank[j] = psum.tile([P, BANK], F32, name="x_bank", tag="pred", bufs=4)
+            for u in range(2):
+                nc.tensor.transpose(x_bank[j][:, u * P : (u + 1) * P], words[:, u : NX // 2 : 2], ident[:])
+
+        def copy_x(j):
+            x_bf[j] = keep.tile([P, 4 * P], BF16, name="x_bf%d" % j, align_bytes=64)
+            nc.vector.tensor_copy(
+                out=x_bf[j][:].bitcast(F32).rearrange("p (r u) -> p r u", u=2),
+                in_=x_bank[j][:, 0 : 2 * P].rearrange("p (u r) -> p r u", u=2),
+            )
+
+        def quantize_x(j):
+            x_codes[j] = keep.tile([P, P], U32, name="x_codes%d" % j, align_bytes=64)
+            x_sc[j] = keep.tile([P, P], U8, name="x_sc%d" % j, align_bytes=64)
+            nc.vector.quantize_mx(out=x_codes[j][:].bitcast(FP8X4), scales=x_sc[j][:], in_=x_bf[j][:])
+
+        limits = keep.tile([P, 16, 4], BF16, name="limits")
+
+        def turn_limits():
+            bank = psum.tile([P, BANK], F32, name="limit_bank", tag="y_turn")
+            words = limit_rows[:].bitcast(F32)
+            for u in range(2):
+                nc.tensor.transpose(bank[:, u * P : (u + 1) * P], words[:, u : BANK // 2 : 2], ident[:])
+            nc.vector.tensor_copy(
+                out=limits[:].bitcast(F32),
+                in_=bank[:, 0 : 2 * P].rearrange("p (u row) -> p row u", u=2)[:, 0:16, :],
+            )
+
+        y_words = keep.tile([P, 2, G * R], U32, name="y_words", align_bytes=64)
+        y_sc = keep.tile([P, 2, G * R], U8, name="y_sc", align_bytes=64)
+
+        u_bank, u_sorted, u_turned, u_low, u_bf, u_codes, u_sc = {}, {}, {}, {}, {}, {}, {}
+        pred, diff, y, y_sorted, y_turned, y_bf = {}, {}, {}, {}, {}, {}
+
+        def input_matmuls(i):
+            g, j = divmod(i, TILES)
+            for h in range(2):
+                u_bank[i, h] = psum.tile([P, BANK], F32, name="u_bank", tag="u_bank", bufs=2)
+                nc.tensor.matmul_mx(
+                    out=u_bank[i, h][:],
+                    lhsT=x_codes[j][:].bitcast(FP8X4),
+                    lhsT_scale=x_sc[j][:],
+                    rhs=gain_w[g][:, h * 2 * BANK : (h + 1) * 2 * BANK].bitcast(FP4X4),
+                    rhs_scale=gain_sc[:, g, h * BANK : (h + 1) * BANK],
+                    start=True,
+                    stop=True,
+                )
+
+        def round_u(i):
+            u_sorted[i] = work.tile([P, NU], BF16, name="u_sorted")
+            for h in range(2):
+                nc.scalar.copy(
+                    out=u_sorted[i][:, h * BANK : (h + 1) * BANK].rearrange("r (u q e) -> r u q e", u=2, e=2),
+                    in_=u_bank[i, h][:].rearrange("r (q u e) -> r u q e", u=2, e=2),
+                )
+
+        def turn_u(i):
+            u_turned[i] = psum.tile([P, BANK], F32, name="u_turned", tag="u_turn")
+            words = u_sorted[i][:].bitcast(F32)
+            for h in range(2):
+                for u in range(2):
+                    src, dst = (2 * h + u) * P, (2 * u + h) * P
+                    nc.tensor.transpose(u_turned[i][:, dst : dst + P], words[:, src : src + P], ident[:])
+
+        def limit_view(first):
+            view = limits[:, first : first + 2, :].rearrange("p h (u e) -> p h u e", e=2)
+            return view.unsqueeze(2).to_broadcast([P, 2, P, 2, 2])
+
+        def upper_limit(i):
+            g = i // TILES
+            u_low[i] = work.tile([P, NU], BF16, name="u_low")
+            nc.vector.tensor_tensor(
+                out=u_low[i][:].rearrange("p (h r u e) -> p h r u e", h=2, u=2, e=2),
+                in0=u_turned[i][:].bitcast(BF16).rearrange("p (u h r e) -> p h r u e", u=2, h=2, e=2),
+                in1=limit_view(2 * g),
+                op=ALU.min,
+            )
+
+        def lower_limit(i):
+            g = i // TILES
+            u_bf[i] = work.tile([P, NU], BF16, name="u_bf", align_bytes=64)
+            nc.vector.tensor_tensor(
+                out=u_bf[i][:].rearrange("p (h r u e) -> p h r u e", h=2, u=2, e=2),
+                in0=u_low[i][:].rearrange("p (h r u e) -> p h r u e", h=2, u=2, e=2),
+                in1=limit_view(8 + 2 * g),
+                op=ALU.max,
+            )
+
+        def quantize_u(i):
+            u_codes[i] = work.tile([P, 2 * P], U32, name="u_codes", bufs=3, align_bytes=64)
+            u_sc[i] = work.tile([P, 2 * P], U8, name="u_sc", bufs=3, align_bytes=64)
+            nc.vector.quantize_mx(out=u_codes[i][:].bitcast(FP8X4), scales=u_sc[i][:], in_=u_bf[i][:])
+
+        def output_matmuls(i):
+            g, j = divmod(i, TILES)
+            for c in range(2):
+                cols = slice(c * BANK, (c + 1) * BANK)
+                byte_cols = slice(c * 2 * BANK, (c + 1) * 2 * BANK)
+                pred[i, c] = psum.tile([P, BANK], F32, name="pred", tag="pred", bufs=4)
+                nc.tensor.matmul_mx(
+                    out=pred[i, c][:],
+                    lhsT=x_codes[j][:].bitcast(FP8X4),
+                    lhsT_scale=x_sc[j][:],
+                    rhs=free_w[g][:, byte_cols].bitcast(FP4X4),
+                    rhs_scale=free_sc[:, g, cols],
+                    start=True,
+                    stop=False,
+                )
+                for h in range(2):
+                    nc.tensor.matmul_mx(
+                        out=pred[i, c][:],
+                        lhsT=u_codes[i][:, h * P : (h + 1) * P].bitcast(FP8X4),
+                        lhsT_scale=u_sc[i][:, h * P : (h + 1) * P],
+                        rhs=forced_w[g][:, h, byte_cols].bitcast(FP4X4),
+                        rhs_scale=forced_sc[:, 2 * g + h, cols],
+                        start=False,
+                        stop=(h == 1),
+                    )
+
+        def subtract_ref(i):
+            j = i % TILES
+            for c in range(2):
+                diff[i, c] = work.tile([P, BANK], F32, name="diff", bufs=4)
+                nc.vector.tensor_tensor(
+                    out=diff[i, c][:], in0=pred[i, c][:], in1=ref_rows[j][:, c * BANK : (c + 1) * BANK], op=ALU.subtract
+                )
+
+        def weigh(i):
+            g, j = divmod(i, TILES)
+            y[i] = work.tile([P, NP], F32, name="y", bufs=4)
+            for c in range(2):
+                cols = slice(c * BANK, (c + 1) * BANK)
+                nc.vector.tensor_tensor(out=y[i][:, cols], in0=diff[i, c][:], in1=w_rows[g][:, cols], op=ALU.mult)
+            nc.sync.dma_start(out=out_0[g, j * P : (j + 1) * P, :], in_=y[i][:])
+
+        def round_y(i):
+            y_sorted[i] = work.tile([P, NP], BF16, name="y_sorted")
+            nc.scalar.copy(
+                out=y_sorted[i][:].rearrange("r (c u q e) -> r c u q e", c=2, u=2, e=2),
+                in_=y[i][:].rearrange("r (c q u e) -> r c u q e", c=2, u=2, e=2),
+            )
+
+        def turn_y(i):
+            y_turned[i] = psum.tile([P, BANK], F32, name="y_turned", tag="y_turn")
+            words = y_sorted[i][:].bitcast(F32)
+            for b in range(4):
+                nc.tensor.transpose(y_turned[i][:, b * P : (b + 1) * P], words[:, b * P : (b + 1) * P], ident[:])
+
+        def copy_y(i):
+            y_bf[i] = work.tile([P, NP], BF16, name="y_bf", align_bytes=64)
+            nc.scalar.copy(
+                out=y_bf[i][:].bitcast(F32).rearrange("p (c r u) -> p c r u", c=2, u=2),
+                in_=y_turned[i][:].rearrange("p (c u r) -> p c r u", c=2, u=2),
+            )
+
+        words_out = out_1.rearrange("c p m t -> p c (m t)").bitcast(I32)
+
+        def store_planes(first, last):
+            cols = slice(first * P, last * P)
+            nc.sync.dma_start(out=words_out[:, :, cols], in_=y_words[:, :, cols].bitcast(I32))
+
+        def store_scales(first, last, queues):
+            cols = slice(first * P, last * P)
+            for q in range(4):
+                queues[q % len(queues)].dma_start(
+                    out=out_2[:, 4 * q : 4 * q + 4, cols].rearrange("c r m -> r c m").bitcast(I32),
+                    in_=y_sc[32 * q : 32 * q + 4, :, cols].bitcast(I32),
+                )
+
+        def quantize_y(i):
+            cols = slice(i * P, (i + 1) * P)
+            for c in range(2):
+                nc.vector.quantize_mx(
+                    out=y_words[:, c, cols].bitcast(FP8X4),
+                    scales=y_sc[:, c, cols],
+                    in_=y_bf[i][:, c * BANK : (c + 1) * BANK],
+                )
+            if i == UNITS - 1:
+                store_planes(i, i + 1)
+                store_scales(i, i + 1, [nc.scalar, nc.sync])
+            elif i == UNITS - 2:
+                store_planes(UNITS - TILES, i + 1)
+                store_scales(0, i + 1, [nc.sync])
+            elif i % TILES == TILES - 1:
+                store_planes(i + 1 - TILES, i + 1)
+
+        def when(stage, i):
+            if 0 <= i < UNITS:
+                stage(i)
+
+        turn_x(0)
+        copy_x(0)
+        quantize_x(0)
+        input_matmuls(0)
+        round_u(0)
+        for j in range(1, TILES):
+            turn_x(j)
+        for j in range(1, TILES):
+            copy_x(j)
+        for j in range(1, TILES):
+            quantize_x(j)
+        turn_limits()
+
+        for s in range(-2, UNITS + 2):
+            when(turn_u, s + 2)
+            when(turn_y, s - 2)
+            when(subtract_ref, s)
+            when(round_y, s - 1)
+            when(input_matmuls, s + 3)
+            when(upper_limit, s + 2)
+            when(weigh, s)
+            when(output_matmuls, s + 1)
+            when(copy_y, s - 2)
+            when(round_u, s + 3)
+            when(lower_limit, s + 2)
+            when(quantize_y, s - 2)
+            when(quantize_u, s + 2)
+            if s in (1, 5):
+                g = (s + 7) // TILES
+                load_gain(g)
+                load_responses(g)
+                load_w(g)

@@ -39,8 +39,8 @@ def tile_condensed_mpc_tracking_error_k7_kernel(
         free_sc = keep.tile([P, G, NP], U8, name="free_sc", align_bytes=64)
         forced_sc = keep.tile([P, 2 * G, NP], U8, name="forced_sc", align_bytes=64)
         limit_rows = keep.tile([P, BANK], BF16, name="limit_rows")
-        nc.vector.memset(gain_sc[:].bitcast(I32), 0)
         nc.vector.memset(limit_rows[:].bitcast(F32), 0.0)
+        nc.vector.memset(gain_sc[:].bitcast(I32), 0)
         nc.vector.memset(free_sc[:].bitcast(I32), 0)
         nc.vector.memset(forced_sc[:].bitcast(I32), 0)
 
@@ -55,9 +55,11 @@ def tile_condensed_mpc_tracking_error_k7_kernel(
             gain_w[g] = keep.tile([P, 2 * NU], U8, name="gain_w%d" % g, align_bytes=64)
             nc.sync.dma_start(out=gain_w[g][:].bitcast(I32), in_=gain_words[g].bitcast(I32))
 
-        def load_responses(g):
+        def load_free(g):
             free_w[g] = keep.tile([P, 2 * NP], U8, name="free_w%d" % g, align_bytes=64)
             nc.sync.dma_start(out=free_w[g][:].bitcast(I32), in_=free_words[g].bitcast(I32))
+
+        def load_forced(g):
             forced_w[g] = keep.tile([P, 2, 2 * NP], U8, name="forced_w%d" % g, align_bytes=64)
             nc.sync.dma_start(
                 out=forced_w[g][:].bitcast(I32),
@@ -78,18 +80,19 @@ def tile_condensed_mpc_tracking_error_k7_kernel(
         load_gain(0)
         load_scales(gain_sc, gain_scales)
         nc.sync.dma_start(out=x_rest[:], in_=x0[P:R, :].rearrange("(j p) k -> p j k", p=P))
-        nc.sync.dma_start(out=limit_rows[0:8, :], in_=u_max.rearrange("g (h k) -> (g h) k", h=2))
-        nc.sync.dma_start(out=limit_rows[8:16, :], in_=u_min.rearrange("g (h k) -> (g h) k", h=2))
+        nc.gpsimd.dma_start(out=limit_rows[0:8, :], in_=u_max.rearrange("g (h k) -> (g h) k", h=2))
+        nc.gpsimd.dma_start(out=limit_rows[8:16, :], in_=u_min.rearrange("g (h k) -> (g h) k", h=2))
+        load_forced(0)
         load_scales(free_sc, free_scales)
         load_scales(forced_sc, forced_scales)
-        load_responses(0)
+        load_free(0)
+        load_gain(1)
         load_ref(0)
         load_w(0)
-        load_ref(1)
-        load_gain(1)
-        load_ref(2)
-        load_ref(3)
-        load_responses(1)
+        for j in range(1, TILES):
+            load_ref(j)
+        load_forced(1)
+        load_free(1)
         load_w(1)
 
         x_codes, x_sc, x_bank, x_bf = {}, {}, {}, {}
@@ -97,7 +100,8 @@ def tile_condensed_mpc_tracking_error_k7_kernel(
         def turn_x(j):
             rows = x_first[:] if j == 0 else x_rest[:, j - 1, :]
             words = rows.bitcast(F32)
-            x_bank[j] = psum.tile([P, BANK], F32, name="x_bank", tag="pred", bufs=4)
+            tag, bufs = [("y_turn", 1), ("pred", 2), ("pred", 2), ("u_turn", 2)][j]
+            x_bank[j] = psum.tile([P, BANK], F32, name="x_bank", tag=tag, bufs=bufs)
             for u in range(2):
                 nc.tensor.transpose(x_bank[j][:, u * P : (u + 1) * P], words[:, u : NX // 2 : 2], ident[:])
 
@@ -113,16 +117,17 @@ def tile_condensed_mpc_tracking_error_k7_kernel(
             x_sc[j] = keep.tile([P, P], U8, name="x_sc%d" % j, align_bytes=64)
             nc.vector.quantize_mx(out=x_codes[j][:].bitcast(FP8X4), scales=x_sc[j][:], in_=x_bf[j][:])
 
-        limits = keep.tile([P, 16, 4], BF16, name="limits")
+        upper = keep.tile([P, 2 * G, 4], BF16, name="upper")
+        limit_bank = psum.tile([P, BANK], F32, name="limit_bank")
+        lower = limit_bank[:].bitcast(BF16).rearrange("p (row s) -> p row s", s=8)[:, 2 * G : 4 * G, 0:4]
 
         def turn_limits():
-            bank = psum.tile([P, BANK], F32, name="limit_bank", tag="y_turn")
             words = limit_rows[:].bitcast(F32)
             for u in range(2):
-                nc.tensor.transpose(bank[:, u * P : (u + 1) * P], words[:, u : BANK // 2 : 2], ident[:])
+                nc.tensor.transpose(limit_bank[:, u:BANK:4], words[:, u : BANK // 2 : 2], ident[:])
             nc.vector.tensor_copy(
-                out=limits[:].bitcast(F32),
-                in_=bank[:, 0 : 2 * P].rearrange("p (u row) -> p row u", u=2)[:, 0:16, :],
+                out=upper[:].bitcast(F32),
+                in_=limit_bank[:].rearrange("p (row s) -> p row s", s=4)[:, 0 : 2 * G, 0:2],
             )
 
         y_words = keep.tile([P, 2, G * R], U32, name="y_words", align_bytes=64)
@@ -154,15 +159,15 @@ def tile_condensed_mpc_tracking_error_k7_kernel(
                 )
 
         def turn_u(i):
-            u_turned[i] = psum.tile([P, BANK], F32, name="u_turned", tag="u_turn")
+            u_turned[i] = psum.tile([P, BANK], F32, name="u_turned", tag="u_turn", bufs=2)
             words = u_sorted[i][:].bitcast(F32)
             for h in range(2):
                 for u in range(2):
                     src, dst = (2 * h + u) * P, (2 * u + h) * P
                     nc.tensor.transpose(u_turned[i][:, dst : dst + P], words[:, src : src + P], ident[:])
 
-        def limit_view(first):
-            view = limits[:, first : first + 2, :].rearrange("p h (u e) -> p h u e", e=2)
+        def limit_view(limits, g):
+            view = limits[:, 2 * g : 2 * g + 2, :].rearrange("p h (u e) -> p h u e", e=2)
             return view.unsqueeze(2).to_broadcast([P, 2, P, 2, 2])
 
         def upper_limit(i):
@@ -171,7 +176,7 @@ def tile_condensed_mpc_tracking_error_k7_kernel(
             nc.vector.tensor_tensor(
                 out=u_low[i][:].rearrange("p (h r u e) -> p h r u e", h=2, u=2, e=2),
                 in0=u_turned[i][:].bitcast(BF16).rearrange("p (u h r e) -> p h r u e", u=2, h=2, e=2),
-                in1=limit_view(2 * g),
+                in1=limit_view(upper, g),
                 op=ALU.min,
             )
 
@@ -180,8 +185,8 @@ def tile_condensed_mpc_tracking_error_k7_kernel(
             u_bf[i] = work.tile([P, NU], BF16, name="u_bf", align_bytes=64)
             nc.vector.tensor_tensor(
                 out=u_bf[i][:].rearrange("p (h r u e) -> p h r u e", h=2, u=2, e=2),
-                in0=u_low[i][:].rearrange("p (h r u e) -> p h r u e", h=2, u=2, e=2),
-                in1=limit_view(8 + 2 * g),
+                in0=limit_view(lower, g),
+                in1=u_low[i][:].rearrange("p (h r u e) -> p h r u e", h=2, u=2, e=2),
                 op=ALU.max,
             )
 
@@ -195,16 +200,7 @@ def tile_condensed_mpc_tracking_error_k7_kernel(
             for c in range(2):
                 cols = slice(c * BANK, (c + 1) * BANK)
                 byte_cols = slice(c * 2 * BANK, (c + 1) * 2 * BANK)
-                pred[i, c] = psum.tile([P, BANK], F32, name="pred", tag="pred", bufs=4)
-                nc.tensor.matmul_mx(
-                    out=pred[i, c][:],
-                    lhsT=x_codes[j][:].bitcast(FP8X4),
-                    lhsT_scale=x_sc[j][:],
-                    rhs=free_w[g][:, byte_cols].bitcast(FP4X4),
-                    rhs_scale=free_sc[:, g, cols],
-                    start=True,
-                    stop=False,
-                )
+                pred[i, c] = psum.tile([P, BANK], F32, name="pred", tag="pred", bufs=2)
                 for h in range(2):
                     nc.tensor.matmul_mx(
                         out=pred[i, c][:],
@@ -212,25 +208,35 @@ def tile_condensed_mpc_tracking_error_k7_kernel(
                         lhsT_scale=u_sc[i][:, h * P : (h + 1) * P],
                         rhs=forced_w[g][:, h, byte_cols].bitcast(FP4X4),
                         rhs_scale=forced_sc[:, 2 * g + h, cols],
-                        start=False,
-                        stop=(h == 1),
+                        start=(h == 0),
+                        stop=False,
                     )
-
-        def subtract_ref(i):
-            j = i % TILES
-            for c in range(2):
-                diff[i, c] = work.tile([P, BANK], F32, name="diff", bufs=4)
-                nc.vector.tensor_tensor(
-                    out=diff[i, c][:], in0=pred[i, c][:], in1=ref_rows[j][:, c * BANK : (c + 1) * BANK], op=ALU.subtract
+                nc.tensor.matmul_mx(
+                    out=pred[i, c][:],
+                    lhsT=x_codes[j][:].bitcast(FP8X4),
+                    lhsT_scale=x_sc[j][:],
+                    rhs=free_w[g][:, byte_cols].bitcast(FP4X4),
+                    rhs_scale=free_sc[:, g, cols],
+                    start=False,
+                    stop=True,
                 )
 
-        def weigh(i):
+        def subtract_ref(i, c):
+            j = i % TILES
+            diff[i, c] = work.tile([P, BANK], F32, name="diff", bufs=4)
+            nc.vector.tensor_tensor(
+                out=diff[i, c][:], in0=pred[i, c][:], in1=ref_rows[j][:, c * BANK : (c + 1) * BANK], op=ALU.subtract
+            )
+
+        def weigh(i, c):
             g, j = divmod(i, TILES)
-            y[i] = work.tile([P, NP], F32, name="y", bufs=4)
-            for c in range(2):
-                cols = slice(c * BANK, (c + 1) * BANK)
-                nc.vector.tensor_tensor(out=y[i][:, cols], in0=diff[i, c][:], in1=w_rows[g][:, cols], op=ALU.mult)
-            nc.sync.dma_start(out=out_0[g, j * P : (j + 1) * P, :], in_=y[i][:])
+            cols = slice(c * BANK, (c + 1) * BANK)
+            if c == 0:
+                y[i] = work.tile([P, NP], F32, name="y", bufs=4)
+            engine = nc.gpsimd if c == 0 else nc.vector
+            engine.tensor_tensor(out=y[i][:, cols], in0=diff[i, c][:], in1=w_rows[g][:, cols], op=ALU.mult)
+            if c == 1:
+                nc.sync.dma_start(out=out_0[g, j * P : (j + 1) * P, :], in_=y[i][:])
 
         def round_y(i):
             y_sorted[i] = work.tile([P, NP], BF16, name="y_sorted")
@@ -283,9 +289,9 @@ def tile_condensed_mpc_tracking_error_k7_kernel(
             elif i % TILES == TILES - 1:
                 store_planes(i + 1 - TILES, i + 1)
 
-        def when(stage, i):
+        def when(stage, i, *more):
             if 0 <= i < UNITS:
-                stage(i)
+                stage(i, *more)
 
         turn_x(0)
         copy_x(0)
@@ -300,22 +306,25 @@ def tile_condensed_mpc_tracking_error_k7_kernel(
             quantize_x(j)
         turn_limits()
 
-        for s in range(-2, UNITS + 2):
-            when(turn_u, s + 2)
+        for s in range(-3, UNITS + 2):
+            when(turn_u, s + 3)
             when(turn_y, s - 2)
-            when(subtract_ref, s)
+            when(subtract_ref, s, 0)
+            when(weigh, s, 0)
             when(round_y, s - 1)
-            when(input_matmuls, s + 3)
+            when(input_matmuls, s + 4)
             when(upper_limit, s + 2)
-            when(weigh, s)
+            when(subtract_ref, s, 1)
+            when(lower_limit, s + 2)
+            when(weigh, s, 1)
             when(output_matmuls, s + 1)
             when(copy_y, s - 2)
-            when(round_u, s + 3)
-            when(lower_limit, s + 2)
+            when(round_u, s + 4)
             when(quantize_y, s - 2)
             when(quantize_u, s + 2)
-            if s in (1, 5):
-                g = (s + 7) // TILES
+            if s in (0, 4):
+                g = s // TILES + 2
                 load_gain(g)
-                load_responses(g)
+                load_forced(g)
+                load_free(g)
                 load_w(g)

@@ -16,9 +16,12 @@ FP4X4 = mybir.dt.float4_e2m1fn_x4
 ALU = mybir.AluOpType
 
 P = 128
-BANK = 512
+HALF = 512
 TILES = R // P
 UNITS = G * TILES
+LEAD = 3
+GPSIMD_COLS = 448
+BANKS = {"u_sums": 2, "u_turned": 1, "pred": 3, "y_turned": 1}
 
 
 def tile_condensed_mpc_tracking_error_k7_kernel(
@@ -32,17 +35,20 @@ def tile_condensed_mpc_tracking_error_k7_kernel(
         psum = ctx.enter_context(tc.psum_pool(name="psum", bufs=1))
         ctx.enter_context(tc.manual_schedule())
 
+        def bank(tag):
+            return psum.tile([P, HALF], F32, name=tag, tag=tag, bufs=BANKS[tag])
+
         ident = keep.tile([P, P], F32, name="ident")
         make_identity(nc, ident[:])
 
         gain_sc = keep.tile([P, G, NU], U8, name="gain_sc", align_bytes=64)
         free_sc = keep.tile([P, G, NP], U8, name="free_sc", align_bytes=64)
         forced_sc = keep.tile([P, 2 * G, NP], U8, name="forced_sc", align_bytes=64)
-        limit_rows = keep.tile([P, BANK], BF16, name="limit_rows")
-        nc.vector.memset(limit_rows[:].bitcast(F32), 0.0)
+        limit_rows = keep.tile([P, HALF], BF16, name="limit_rows")
         nc.vector.memset(gain_sc[:].bitcast(I32), 0)
-        nc.vector.memset(free_sc[:].bitcast(I32), 0)
+        nc.vector.memset(limit_rows[:].bitcast(F32), 0.0)
         nc.vector.memset(forced_sc[:].bitcast(I32), 0)
+        nc.vector.memset(free_sc[:].bitcast(I32), 0)
 
         def load_scales(plane, rows):
             by_row = rows.rearrange("g (q r) n -> r q g n", r=4)
@@ -80,72 +86,61 @@ def tile_condensed_mpc_tracking_error_k7_kernel(
         load_gain(0)
         load_scales(gain_sc, gain_scales)
         nc.sync.dma_start(out=x_rest[:], in_=x0[P:R, :].rearrange("(j p) k -> p j k", p=P))
-        nc.gpsimd.dma_start(out=limit_rows[0:8, :], in_=u_max.rearrange("g (h k) -> (g h) k", h=2))
-        nc.gpsimd.dma_start(out=limit_rows[8:16, :], in_=u_min.rearrange("g (h k) -> (g h) k", h=2))
-        load_forced(0)
-        load_scales(free_sc, free_scales)
+        nc.sync.dma_start(out=limit_rows[0 : 2 * G, :], in_=u_max.rearrange("g (h k) -> (g h) k", h=2))
+        nc.sync.dma_start(out=limit_rows[2 * G : 4 * G, :], in_=u_min.rearrange("g (h k) -> (g h) k", h=2))
         load_scales(forced_sc, forced_scales)
+        load_scales(free_sc, free_scales)
+        load_forced(0)
         load_free(0)
-        load_gain(1)
         load_ref(0)
         load_w(0)
+        load_gain(1)
         for j in range(1, TILES):
             load_ref(j)
         load_forced(1)
         load_free(1)
         load_w(1)
 
-        x_codes, x_sc, x_bank, x_bf = {}, {}, {}, {}
+        x_codes, x_sc = {}, {}
 
-        def turn_x(j):
-            rows = x_first[:] if j == 0 else x_rest[:, j - 1, :]
+        def quantize_x(j, rows, turned, copy):
             words = rows.bitcast(F32)
-            tag, bufs = [("y_turn", 1), ("pred", 2), ("pred", 2), ("u_turn", 2)][j]
-            x_bank[j] = psum.tile([P, BANK], F32, name="x_bank", tag=tag, bufs=bufs)
             for u in range(2):
-                nc.tensor.transpose(x_bank[j][:, u * P : (u + 1) * P], words[:, u : NX // 2 : 2], ident[:])
-
-        def copy_x(j):
-            x_bf[j] = keep.tile([P, 4 * P], BF16, name="x_bf%d" % j, align_bytes=64)
-            nc.vector.tensor_copy(
-                out=x_bf[j][:].bitcast(F32).rearrange("p (r u) -> p r u", u=2),
-                in_=x_bank[j][:, 0 : 2 * P].rearrange("p (u r) -> p r u", u=2),
+                nc.tensor.transpose(turned[:, u * P : (u + 1) * P], words[:, u : NX // 2 : 2], ident[:])
+            x_bf = keep.tile([P, 4 * P], BF16, name="x_bf%d" % j, align_bytes=64)
+            copy(
+                out=x_bf[:].bitcast(F32).rearrange("p (r u) -> p r u", u=2),
+                in_=turned[:, 0 : 2 * P].rearrange("p (u r) -> p r u", u=2),
             )
-
-        def quantize_x(j):
             x_codes[j] = keep.tile([P, P], U32, name="x_codes%d" % j, align_bytes=64)
             x_sc[j] = keep.tile([P, P], U8, name="x_sc%d" % j, align_bytes=64)
-            nc.vector.quantize_mx(out=x_codes[j][:].bitcast(FP8X4), scales=x_sc[j][:], in_=x_bf[j][:])
+            nc.vector.quantize_mx(out=x_codes[j][:].bitcast(FP8X4), scales=x_sc[j][:], in_=x_bf[:])
 
+        limit_bank = psum.tile([P, HALF], F32, name="limit_bank")
         upper = keep.tile([P, 2 * G, 4], BF16, name="upper")
-        limit_bank = psum.tile([P, BANK], F32, name="limit_bank")
         lower = limit_bank[:].bitcast(BF16).rearrange("p (row s) -> p row s", s=8)[:, 2 * G : 4 * G, 0:4]
 
         def turn_limits():
             words = limit_rows[:].bitcast(F32)
             for u in range(2):
-                nc.tensor.transpose(limit_bank[:, u:BANK:4], words[:, u : BANK // 2 : 2], ident[:])
+                nc.tensor.transpose(limit_bank[:, u:HALF:4], words[:, u : HALF // 2 : 2], ident[:])
             nc.vector.tensor_copy(
                 out=upper[:].bitcast(F32),
                 in_=limit_bank[:].rearrange("p (row s) -> p row s", s=4)[:, 0 : 2 * G, 0:2],
             )
 
-        y_words = keep.tile([P, 2, G * R], U32, name="y_words", align_bytes=64)
-        y_sc = keep.tile([P, 2, G * R], U8, name="y_sc", align_bytes=64)
+        u_sums, u_sorted, u_turned, u_capped, u_bf, u_codes, u_sc = {}, {}, {}, {}, {}, {}, {}
 
-        u_bank, u_sorted, u_turned, u_low, u_bf, u_codes, u_sc = {}, {}, {}, {}, {}, {}, {}
-        pred, diff, y, y_sorted, y_turned, y_bf = {}, {}, {}, {}, {}, {}
-
-        def input_matmuls(i):
+        def gain_matmuls(i, tag="u_sums"):
             g, j = divmod(i, TILES)
             for h in range(2):
-                u_bank[i, h] = psum.tile([P, BANK], F32, name="u_bank", tag="u_bank", bufs=2)
+                u_sums[i, h] = bank(tag)
                 nc.tensor.matmul_mx(
-                    out=u_bank[i, h][:],
+                    out=u_sums[i, h][:],
                     lhsT=x_codes[j][:].bitcast(FP8X4),
                     lhsT_scale=x_sc[j][:],
-                    rhs=gain_w[g][:, h * 2 * BANK : (h + 1) * 2 * BANK].bitcast(FP4X4),
-                    rhs_scale=gain_sc[:, g, h * BANK : (h + 1) * BANK],
+                    rhs=gain_w[g][:, h * 2 * HALF : (h + 1) * 2 * HALF].bitcast(FP4X4),
+                    rhs_scale=gain_sc[:, g, h * HALF : (h + 1) * HALF],
                     start=True,
                     stop=True,
                 )
@@ -154,114 +149,141 @@ def tile_condensed_mpc_tracking_error_k7_kernel(
             u_sorted[i] = work.tile([P, NU], BF16, name="u_sorted")
             for h in range(2):
                 nc.scalar.copy(
-                    out=u_sorted[i][:, h * BANK : (h + 1) * BANK].rearrange("r (u q e) -> r u q e", u=2, e=2),
-                    in_=u_bank[i, h][:].rearrange("r (q u e) -> r u q e", u=2, e=2),
+                    out=u_sorted[i][:, h * HALF : (h + 1) * HALF].rearrange("r (u p e) -> r u p e", u=2, e=2),
+                    in_=u_sums[i, h][:].rearrange("r (p u e) -> r u p e", u=2, e=2),
                 )
 
-        def turn_u(i):
-            u_turned[i] = psum.tile([P, BANK], F32, name="u_turned", tag="u_turn", bufs=2)
+        def turn_u(i, tag="u_turned"):
+            u_turned[i] = bank(tag)
             words = u_sorted[i][:].bitcast(F32)
             for h in range(2):
                 for u in range(2):
                     src, dst = (2 * h + u) * P, (2 * u + h) * P
                     nc.tensor.transpose(u_turned[i][:, dst : dst + P], words[:, src : src + P], ident[:])
 
-        def limit_view(limits, g):
+        def by_state(tile):
+            return tile[:].rearrange("p (h r u e) -> p h r u e", h=2, u=2, e=2)
+
+        def for_all_states(limits, g):
             view = limits[:, 2 * g : 2 * g + 2, :].rearrange("p h (u e) -> p h u e", e=2)
             return view.unsqueeze(2).to_broadcast([P, 2, P, 2, 2])
 
-        def upper_limit(i):
-            g = i // TILES
-            u_low[i] = work.tile([P, NU], BF16, name="u_low")
+        def apply_upper(i):
+            u_capped[i] = work.tile([P, NU], BF16, name="u_capped")
             nc.vector.tensor_tensor(
-                out=u_low[i][:].rearrange("p (h r u e) -> p h r u e", h=2, u=2, e=2),
+                out=by_state(u_capped[i]),
                 in0=u_turned[i][:].bitcast(BF16).rearrange("p (u h r e) -> p h r u e", u=2, h=2, e=2),
-                in1=limit_view(upper, g),
+                in1=for_all_states(upper, i // TILES),
                 op=ALU.min,
             )
 
-        def lower_limit(i):
-            g = i // TILES
+        def apply_lower(i):
             u_bf[i] = work.tile([P, NU], BF16, name="u_bf", align_bytes=64)
             nc.vector.tensor_tensor(
-                out=u_bf[i][:].rearrange("p (h r u e) -> p h r u e", h=2, u=2, e=2),
-                in0=limit_view(lower, g),
-                in1=u_low[i][:].rearrange("p (h r u e) -> p h r u e", h=2, u=2, e=2),
-                op=ALU.max,
+                out=by_state(u_bf[i]), in0=for_all_states(lower, i // TILES), in1=by_state(u_capped[i]), op=ALU.max
             )
 
         def quantize_u(i):
-            u_codes[i] = work.tile([P, 2 * P], U32, name="u_codes", bufs=3, align_bytes=64)
-            u_sc[i] = work.tile([P, 2 * P], U8, name="u_sc", bufs=3, align_bytes=64)
+            u_codes[i] = work.tile([P, 2 * P], U32, name="u_codes", bufs=LEAD + 1, align_bytes=64)
+            u_sc[i] = work.tile([P, 2 * P], U8, name="u_sc", bufs=LEAD + 1, align_bytes=64)
             nc.vector.quantize_mx(out=u_codes[i][:].bitcast(FP8X4), scales=u_sc[i][:], in_=u_bf[i][:])
 
-        def output_matmuls(i):
+        pred, diff, y, y_sorted, y_turned, y_bf = {}, {}, {}, {}, {}, {}
+
+        def response_matmuls(i, c):
             g, j = divmod(i, TILES)
-            for c in range(2):
-                cols = slice(c * BANK, (c + 1) * BANK)
-                byte_cols = slice(c * 2 * BANK, (c + 1) * 2 * BANK)
-                pred[i, c] = psum.tile([P, BANK], F32, name="pred", tag="pred", bufs=2)
-                for h in range(2):
-                    nc.tensor.matmul_mx(
-                        out=pred[i, c][:],
-                        lhsT=u_codes[i][:, h * P : (h + 1) * P].bitcast(FP8X4),
-                        lhsT_scale=u_sc[i][:, h * P : (h + 1) * P],
-                        rhs=forced_w[g][:, h, byte_cols].bitcast(FP4X4),
-                        rhs_scale=forced_sc[:, 2 * g + h, cols],
-                        start=(h == 0),
-                        stop=False,
-                    )
+            cols = slice(c * HALF, (c + 1) * HALF)
+            byte_cols = slice(c * 2 * HALF, (c + 1) * 2 * HALF)
+            pred[i, c] = bank("pred")
+            for h in range(2):
                 nc.tensor.matmul_mx(
                     out=pred[i, c][:],
-                    lhsT=x_codes[j][:].bitcast(FP8X4),
-                    lhsT_scale=x_sc[j][:],
-                    rhs=free_w[g][:, byte_cols].bitcast(FP4X4),
-                    rhs_scale=free_sc[:, g, cols],
-                    start=False,
-                    stop=True,
+                    lhsT=u_codes[i][:, h * P : (h + 1) * P].bitcast(FP8X4),
+                    lhsT_scale=u_sc[i][:, h * P : (h + 1) * P],
+                    rhs=forced_w[g][:, h, byte_cols].bitcast(FP4X4),
+                    rhs_scale=forced_sc[:, 2 * g + h, cols],
+                    start=(h == 0),
+                    stop=False,
                 )
+            nc.tensor.matmul_mx(
+                out=pred[i, c][:],
+                lhsT=x_codes[j][:].bitcast(FP8X4),
+                lhsT_scale=x_sc[j][:],
+                rhs=free_w[g][:, byte_cols].bitcast(FP4X4),
+                rhs_scale=free_sc[:, g, cols],
+                start=False,
+                stop=True,
+            )
 
         def subtract_ref(i, c):
-            j = i % TILES
-            diff[i, c] = work.tile([P, BANK], F32, name="diff", bufs=4)
-            nc.vector.tensor_tensor(
-                out=diff[i, c][:], in0=pred[i, c][:], in1=ref_rows[j][:, c * BANK : (c + 1) * BANK], op=ALU.subtract
-            )
-
-        def weigh(i, c):
-            g, j = divmod(i, TILES)
-            cols = slice(c * BANK, (c + 1) * BANK)
+            cols = slice(c * HALF, (c + 1) * HALF)
             if c == 0:
+                diff[i] = work.tile([P, NP], F32, name="diff", bufs=3)
                 y[i] = work.tile([P, NP], F32, name="y", bufs=4)
-            engine = nc.gpsimd if c == 0 else nc.vector
-            engine.tensor_tensor(out=y[i][:, cols], in0=diff[i, c][:], in1=w_rows[g][:, cols], op=ALU.mult)
-            if c == 1:
-                nc.sync.dma_start(out=out_0[g, j * P : (j + 1) * P, :], in_=y[i][:])
-
-        def round_y(i):
-            y_sorted[i] = work.tile([P, NP], BF16, name="y_sorted")
-            nc.scalar.copy(
-                out=y_sorted[i][:].rearrange("r (c u q e) -> r c u q e", c=2, u=2, e=2),
-                in_=y[i][:].rearrange("r (c q u e) -> r c u q e", c=2, u=2, e=2),
+            nc.vector.tensor_tensor(
+                out=diff[i][:, cols], in0=pred[i, c][:], in1=ref_rows[i % TILES][:, cols], op=ALU.subtract
             )
 
-        def turn_y(i):
-            y_turned[i] = psum.tile([P, BANK], F32, name="y_turned", tag="y_turn")
-            words = y_sorted[i][:].bitcast(F32)
-            for b in range(4):
-                nc.tensor.transpose(y_turned[i][:, b * P : (b + 1) * P], words[:, b * P : (b + 1) * P], ident[:])
+        def weigh(engine, i, cols):
+            engine.tensor_tensor(out=y[i][:, cols], in0=diff[i][:, cols], in1=w_rows[i // TILES][:, cols], op=ALU.mult)
 
-        def copy_y(i):
-            y_bf[i] = work.tile([P, NP], BF16, name="y_bf", align_bytes=64)
-            nc.scalar.copy(
-                out=y_bf[i][:].bitcast(F32).rearrange("p (c r u) -> p c r u", c=2, u=2),
-                in_=y_turned[i][:].rearrange("p (c u r) -> p c r u", c=2, u=2),
+        def store_y(i, cols):
+            g, j = divmod(i, TILES)
+            nc.sync.dma_start(out=out_0[g, j * P : (j + 1) * P, cols], in_=y[i][:, cols])
+
+        def weigh_on_gpsimd(i):
+            weigh(nc.gpsimd, i, slice(0, GPSIMD_COLS))
+
+        def weigh_rest_and_store(i):
+            weigh(nc.vector, i, slice(GPSIMD_COLS, NP))
+            store_y(i, slice(0, NP))
+
+        def round_y(i, copy, first=0, last=NP // 16):
+            if first == 0:
+                y_sorted[i] = work.tile([P, NP], BF16, name="y_sorted")
+            copy(
+                out=y_sorted[i][:].rearrange("r (u s n e) -> r s u n e", u=2, n=4, e=2)[:, first:last],
+                in_=y[i][:].rearrange("r (s n u e) -> r s u n e", n=4, u=2, e=2)[:, first:last],
+            )
+
+        def turn_y(i, tag="y_turned"):
+            y_turned[i] = bank(tag)
+            words = y_sorted[i][:].bitcast(F32)
+            for run in range(4):
+                cols = slice(run * P, (run + 1) * P)
+                nc.tensor.transpose(y_turned[i][:, cols], words[:, cols], ident[:])
+
+        def batch_units(batch):
+            return range(max(2 * batch - 1, 0), min(2 * batch + 1, UNITS))
+
+        def interleave_y(i, copy):
+            batch = (i + 1) // 2
+            place = i - batch_units(batch).start
+            if place == 0:
+                y_bf[batch] = work.tile([P, 2, 2 * 4 * P], BF16, name="y_bf", bufs=3, align_bytes=64)
+            words = y_bf[batch][:].bitcast(F32)[:, :, place * 2 * P : (place + 1) * 2 * P]
+            copy(
+                out=words.rearrange("p c (r u) -> p c r u", u=2),
+                in_=y_turned[i][:].rearrange("p (u c r) -> p c r u", u=2, c=2),
+            )
+
+        y_words = keep.tile([P, 2, G * R], U32, name="y_words", align_bytes=64)
+        y_sc = keep.tile([P, 2, G * R], U8, name="y_sc", align_bytes=64)
+
+        def quantize_y(batch, c):
+            units = batch_units(batch)
+            cols = slice(units.start * P, units.stop * P)
+            nc.vector.quantize_mx(
+                out=y_words[:, c, cols].bitcast(FP8X4),
+                scales=y_sc[:, c, cols],
+                in_=y_bf[batch][:, c, 0 : len(units) * 4 * P],
             )
 
         words_out = out_1.rearrange("c p m t -> p c (m t)").bitcast(I32)
 
-        def store_planes(first, last):
-            cols = slice(first * P, last * P)
+        def store_words(batch):
+            units = batch_units(batch)
+            cols = slice(units.start * P, units.stop * P)
             nc.sync.dma_start(out=words_out[:, :, cols], in_=y_words[:, :, cols].bitcast(I32))
 
         def store_scales(first, last, queues):
@@ -272,59 +294,112 @@ def tile_condensed_mpc_tracking_error_k7_kernel(
                     in_=y_sc[32 * q : 32 * q + 4, :, cols].bitcast(I32),
                 )
 
-        def quantize_y(i):
-            cols = slice(i * P, (i + 1) * P)
-            for c in range(2):
-                nc.vector.quantize_mx(
-                    out=y_words[:, c, cols].bitcast(FP8X4),
-                    scales=y_sc[:, c, cols],
-                    in_=y_bf[i][:, c * BANK : (c + 1) * BANK],
-                )
-            if i == UNITS - 1:
-                store_planes(i, i + 1)
-                store_scales(i, i + 1, [nc.scalar, nc.sync])
-            elif i == UNITS - 2:
-                store_planes(UNITS - TILES, i + 1)
-                store_scales(0, i + 1, [nc.sync])
-            elif i % TILES == TILES - 1:
-                store_planes(i + 1 - TILES, i + 1)
-
-        def when(stage, i, *more):
-            if 0 <= i < UNITS:
-                stage(i, *more)
-
-        turn_x(0)
-        copy_x(0)
-        quantize_x(0)
-        input_matmuls(0)
+        quantize_x(0, x_first[:], bank("y_turned"), nc.vector.tensor_copy)
+        for j in range(1, TILES):
+            quantize_x(j, x_rest[:, j - 1, :], bank("pred"), nc.scalar.copy)
+        gain_matmuls(0)
         round_u(0)
-        for j in range(1, TILES):
-            turn_x(j)
-        for j in range(1, TILES):
-            copy_x(j)
-        for j in range(1, TILES):
-            quantize_x(j)
+        gain_matmuls(1, "pred")
+        round_u(1)
         turn_limits()
+        turn_u(0)
+        gain_matmuls(2)
+        turn_u(1, "y_turned")
+        apply_upper(0)
+        apply_upper(1)
+        apply_lower(0)
+        apply_lower(1)
+        quantize_u(0)
+        round_u(2)
+        turn_u(2)
+        gain_matmuls(3)
+        round_u(3)
+        response_matmuls(0, 0)
+        response_matmuls(0, 1)
+        apply_upper(2)
+        quantize_u(1)
+        apply_lower(2)
 
-        for s in range(-3, UNITS + 2):
-            when(turn_u, s + 3)
-            when(turn_y, s - 2)
-            when(subtract_ref, s, 0)
-            when(weigh, s, 0)
-            when(round_y, s - 1)
-            when(input_matmuls, s + 4)
-            when(upper_limit, s + 2)
-            when(subtract_ref, s, 1)
-            when(lower_limit, s + 2)
-            when(weigh, s, 1)
-            when(output_matmuls, s + 1)
-            when(copy_y, s - 2)
-            when(round_u, s + 4)
-            when(quantize_y, s - 2)
-            when(quantize_u, s + 2)
-            if s in (0, 4):
+        for s in range(UNITS - LEAD):
+            turn_u(s + LEAD)
+            if s >= 2:
+                turn_y(s - 2)
+            subtract_ref(s, 0)
+            if s == 0:
+                quantize_u(LEAD - 1)
+            weigh_on_gpsimd(s)
+            if s >= 1:
+                round_y(s - 1, nc.scalar.copy)
+            if s + LEAD + 1 < UNITS:
+                gain_matmuls(s + LEAD + 1)
+            apply_upper(s + LEAD)
+            subtract_ref(s, 1)
+            apply_lower(s + LEAD)
+            weigh_rest_and_store(s)
+            response_matmuls(s + 1, 0)
+            response_matmuls(s + 1, 1)
+            if s >= 2:
+                interleave_y(s - 2, nc.scalar.copy)
+            if s + LEAD + 1 < UNITS:
+                round_u(s + LEAD + 1)
+            if s >= 2:
+                batch, c = divmod(s - 2, 2)
+                quantize_y(batch, c)
+                if c == 1:
+                    store_words(batch)
+            quantize_u(s + LEAD)
+            if s in (0, TILES):
                 g = s // TILES + 2
                 load_gain(g)
                 load_forced(g)
                 load_free(g)
                 load_w(g)
+
+        a, b, z = UNITS - 3, UNITS - 2, UNITS - 1
+        last_batch = UNITS // 2
+        quantize_y(last_batch - 3, 1)
+        store_words(last_batch - 3)
+        early_units = batch_units(last_batch - 3).stop
+        store_scales(0, early_units, [nc.sync])
+        subtract_ref(a, 0)
+        weigh_on_gpsimd(a)
+        round_y(a - 1, nc.scalar.copy)
+        turn_y(a - 2)
+        interleave_y(a - 2, nc.scalar.copy)
+        response_matmuls(b, 0)
+        subtract_ref(a, 1)
+        response_matmuls(b, 1)
+        subtract_ref(b, 0)
+        turn_y(a - 1)
+        interleave_y(a - 1, nc.scalar.copy)
+        response_matmuls(z, 0)
+        weigh_rest_and_store(a)
+        weigh_on_gpsimd(b)
+        round_y(a, nc.scalar.copy)
+        subtract_ref(b, 1)
+        response_matmuls(z, 1)
+        subtract_ref(z, 0)
+        turn_y(a)
+        weigh_rest_and_store(b)
+        round_y(b, nc.scalar.copy)
+        interleave_y(a, nc.scalar.copy)
+        subtract_ref(z, 1)
+        for c in range(2):
+            weigh(nc.vector, z, slice(c * HALF, (c + 1) * HALF))
+            store_y(z, slice(c * HALF, (c + 1) * HALF))
+        for c in range(2):
+            round_y(z, nc.vector.tensor_copy, c * HALF // 16, (c + 1) * HALF // 16)
+        turn_y(b, "u_turned")
+        interleave_y(b, nc.scalar.copy)
+        for c in range(2):
+            quantize_y(last_batch - 2, c)
+        store_words(last_batch - 2)
+        turn_y(z, "u_sums")
+        interleave_y(z, nc.vector.tensor_copy)
+        for c in range(2):
+            quantize_y(last_batch - 1, c)
+        store_words(last_batch - 1)
+        for c in range(2):
+            quantize_y(last_batch, c)
+        store_words(last_batch)
+        store_scales(early_units, UNITS, [nc.scalar, nc.sync])

from contextlib import ExitStack

import concourse.mybir as mybir
from concourse.masks import make_identity

G, R, NX, NU, NP = 4, 512, 512, 1024, 1024
FLOPS = 2 * G * R * (NX * NU + NX * NP + NU * NP)

F32 = mybir.dt.float32
BF16 = mybir.dt.bfloat16
I32 = mybir.dt.int32
U32 = mybir.dt.uint32
U8 = mybir.dt.uint8
FP8X4 = mybir.dt.float8_e4m3fn_x4
FP4X4 = mybir.dt.float4_e2m1fn_x4
ALU = mybir.AluOpType

P = 128
HALF = 512
TILES = R // P
UNITS = G * TILES
LEAD = 3
GPSIMD_COLS = 448
BANKS = {"u_sums": 2, "u_turned": 1, "pred": 3, "y_turned": 1}


def tile_condensed_mpc_tracking_error_k7_kernel(
    tc, x0, gain_words, gain_scales, free_words, free_scales, forced_words, forced_scales,
    u_max, u_min, ref, w, out_0, out_1, out_2,
):
    nc = tc.nc
    with ExitStack() as ctx:
        keep = ctx.enter_context(tc.tile_pool(name="keep", bufs=1))
        work = ctx.enter_context(tc.tile_pool(name="work", bufs=2))
        psum = ctx.enter_context(tc.psum_pool(name="psum", bufs=1))
        ctx.enter_context(tc.manual_schedule())

        def bank(tag):
            return psum.tile([P, HALF], F32, name=tag, tag=tag, bufs=BANKS[tag])

        ident = keep.tile([P, P], F32, name="ident")
        make_identity(nc, ident[:])

        gain_sc = keep.tile([P, G, NU], U8, name="gain_sc", align_bytes=64)
        free_sc = keep.tile([P, G, NP], U8, name="free_sc", align_bytes=64)
        forced_sc = keep.tile([P, 2 * G, NP], U8, name="forced_sc", align_bytes=64)
        limit_rows = keep.tile([P, HALF], BF16, name="limit_rows")
        nc.vector.memset(gain_sc[:].bitcast(I32), 0)
        nc.vector.memset(limit_rows[:].bitcast(F32), 0.0)
        nc.vector.memset(forced_sc[:].bitcast(I32), 0)
        nc.vector.memset(free_sc[:].bitcast(I32), 0)

        def load_scales(plane, rows):
            by_row = rows.rearrange("g (q r) n -> r q g n", r=4)
            for r in range(4):
                nc.sync.dma_start(out=plane[r:P:32, :, :].bitcast(I32), in_=by_row[r].bitcast(I32))

        gain_w, free_w, forced_w, w_rows, ref_rows = {}, {}, {}, {}, {}

        def load_gain(g):
            gain_w[g] = keep.tile([P, 2 * NU], U8, name="gain_w%d" % g, align_bytes=64)
            nc.sync.dma_start(out=gain_w[g][:].bitcast(I32), in_=gain_words[g].bitcast(I32))

        def load_free(g):
            free_w[g] = keep.tile([P, 2 * NP], U8, name="free_w%d" % g, align_bytes=64)
            nc.sync.dma_start(out=free_w[g][:].bitcast(I32), in_=free_words[g].bitcast(I32))

        def load_forced(g):
            forced_w[g] = keep.tile([P, 2, 2 * NP], U8, name="forced_w%d" % g, align_bytes=64)
            nc.sync.dma_start(
                out=forced_w[g][:].bitcast(I32),
                in_=forced_words[2 * g : 2 * g + 2].rearrange("h p n -> p h n").bitcast(I32),
            )

        def load_w(g):
            w_rows[g] = keep.tile([P, NP], BF16, name="w_rows%d" % g)
            nc.sync.dma_start(out=w_rows[g][:], in_=w[g].partition_broadcast(P))

        def load_ref(j):
            ref_rows[j] = keep.tile([P, NP], BF16, name="ref_rows%d" % j)
            nc.sync.dma_start(out=ref_rows[j][:], in_=ref[j * P : (j + 1) * P, :])

        x_first = keep.tile([P, NX], BF16, name="x_first")
        x_rest = keep.tile([P, TILES - 1, NX], BF16, name="x_rest")
        nc.sync.dma_start(out=x_first[:], in_=x0[0:P, :])
        load_gain(0)
        load_scales(gain_sc, gain_scales)
        nc.sync.dma_start(out=x_rest[:], in_=x0[P:R, :].rearrange("(j p) k -> p j k", p=P))
        nc.sync.dma_start(out=limit_rows[0 : 2 * G, :], in_=u_max.rearrange("g (h k) -> (g h) k", h=2))
        nc.sync.dma_start(out=limit_rows[2 * G : 4 * G, :], in_=u_min.rearrange("g (h k) -> (g h) k", h=2))
        load_scales(forced_sc, forced_scales)
        load_scales(free_sc, free_scales)
        load_forced(0)
        load_free(0)
        load_ref(0)
        load_w(0)
        load_gain(1)
        for j in range(1, TILES):
            load_ref(j)
        load_forced(1)
        load_free(1)
        load_w(1)

        x_codes, x_sc = {}, {}

        def quantize_x(j, rows, turned, copy):
            words = rows.bitcast(F32)
            for u in range(2):
                nc.tensor.transpose(turned[:, u * P : (u + 1) * P], words[:, u : NX // 2 : 2], ident[:])
            x_bf = keep.tile([P, 4 * P], BF16, name="x_bf%d" % j, align_bytes=64)
            copy(
                out=x_bf[:].bitcast(F32).rearrange("p (r u) -> p r u", u=2),
                in_=turned[:, 0 : 2 * P].rearrange("p (u r) -> p r u", u=2),
            )
            x_codes[j] = keep.tile([P, P], U32, name="x_codes%d" % j, align_bytes=64)
            x_sc[j] = keep.tile([P, P], U8, name="x_sc%d" % j, align_bytes=64)
            nc.vector.quantize_mx(out=x_codes[j][:].bitcast(FP8X4), scales=x_sc[j][:], in_=x_bf[:])

        limit_bank = psum.tile([P, HALF], F32, name="limit_bank")
        upper = keep.tile([P, 2 * G, 4], BF16, name="upper")
        lower = limit_bank[:].bitcast(BF16).rearrange("p (row s) -> p row s", s=8)[:, 2 * G : 4 * G, 0:4]

        def turn_limits():
            words = limit_rows[:].bitcast(F32)
            for u in range(2):
                nc.tensor.transpose(limit_bank[:, u:HALF:4], words[:, u : HALF // 2 : 2], ident[:])
            nc.vector.tensor_copy(
                out=upper[:].bitcast(F32),
                in_=limit_bank[:].rearrange("p (row s) -> p row s", s=4)[:, 0 : 2 * G, 0:2],
            )

        u_sums, u_sorted, u_turned, u_capped, u_bf, u_codes, u_sc = {}, {}, {}, {}, {}, {}, {}

        def gain_matmuls(i, tag="u_sums"):
            g, j = divmod(i, TILES)
            for h in range(2):
                u_sums[i, h] = bank(tag)
                nc.tensor.matmul_mx(
                    out=u_sums[i, h][:],
                    lhsT=x_codes[j][:].bitcast(FP8X4),
                    lhsT_scale=x_sc[j][:],
                    rhs=gain_w[g][:, h * 2 * HALF : (h + 1) * 2 * HALF].bitcast(FP4X4),
                    rhs_scale=gain_sc[:, g, h * HALF : (h + 1) * HALF],
                    start=True,
                    stop=True,
                )

        def round_u(i):
            u_sorted[i] = work.tile([P, NU], BF16, name="u_sorted")
            for h in range(2):
                nc.scalar.copy(
                    out=u_sorted[i][:, h * HALF : (h + 1) * HALF].rearrange("r (u p e) -> r u p e", u=2, e=2),
                    in_=u_sums[i, h][:].rearrange("r (p u e) -> r u p e", u=2, e=2),
                )

        def turn_u(i, tag="u_turned"):
            u_turned[i] = bank(tag)
            words = u_sorted[i][:].bitcast(F32)
            for h in range(2):
                for u in range(2):
                    src, dst = (2 * h + u) * P, (2 * u + h) * P
                    nc.tensor.transpose(u_turned[i][:, dst : dst + P], words[:, src : src + P], ident[:])

        def by_state(tile):
            return tile[:].rearrange("p (h r u e) -> p h r u e", h=2, u=2, e=2)

        def for_all_states(limits, g):
            view = limits[:, 2 * g : 2 * g + 2, :].rearrange("p h (u e) -> p h u e", e=2)
            return view.unsqueeze(2).to_broadcast([P, 2, P, 2, 2])

        def apply_upper(i):
            u_capped[i] = work.tile([P, NU], BF16, name="u_capped")
            nc.vector.tensor_tensor(
                out=by_state(u_capped[i]),
                in0=u_turned[i][:].bitcast(BF16).rearrange("p (u h r e) -> p h r u e", u=2, h=2, e=2),
                in1=for_all_states(upper, i // TILES),
                op=ALU.min,
            )

        def apply_lower(i):
            u_bf[i] = work.tile([P, NU], BF16, name="u_bf", align_bytes=64)
            nc.vector.tensor_tensor(
                out=by_state(u_bf[i]), in0=for_all_states(lower, i // TILES), in1=by_state(u_capped[i]), op=ALU.max
            )

        def quantize_u(i):
            u_codes[i] = work.tile([P, 2 * P], U32, name="u_codes", bufs=LEAD + 1, align_bytes=64)
            u_sc[i] = work.tile([P, 2 * P], U8, name="u_sc", bufs=LEAD + 1, align_bytes=64)
            nc.vector.quantize_mx(out=u_codes[i][:].bitcast(FP8X4), scales=u_sc[i][:], in_=u_bf[i][:])

        pred, diff, y, y_sorted, y_turned, y_bf = {}, {}, {}, {}, {}, {}

        def response_matmuls(i, c):
            g, j = divmod(i, TILES)
            cols = slice(c * HALF, (c + 1) * HALF)
            byte_cols = slice(c * 2 * HALF, (c + 1) * 2 * HALF)
            pred[i, c] = bank("pred")
            for h in range(2):
                nc.tensor.matmul_mx(
                    out=pred[i, c][:],
                    lhsT=u_codes[i][:, h * P : (h + 1) * P].bitcast(FP8X4),
                    lhsT_scale=u_sc[i][:, h * P : (h + 1) * P],
                    rhs=forced_w[g][:, h, byte_cols].bitcast(FP4X4),
                    rhs_scale=forced_sc[:, 2 * g + h, cols],
                    start=(h == 0),
                    stop=False,
                )
            nc.tensor.matmul_mx(
                out=pred[i, c][:],
                lhsT=x_codes[j][:].bitcast(FP8X4),
                lhsT_scale=x_sc[j][:],
                rhs=free_w[g][:, byte_cols].bitcast(FP4X4),
                rhs_scale=free_sc[:, g, cols],
                start=False,
                stop=True,
            )

        def subtract_ref(i, c):
            cols = slice(c * HALF, (c + 1) * HALF)
            if c == 0:
                diff[i] = work.tile([P, NP], F32, name="diff", bufs=3)
                y[i] = work.tile([P, NP], F32, name="y", bufs=4)
            nc.vector.tensor_tensor(
                out=diff[i][:, cols], in0=pred[i, c][:], in1=ref_rows[i % TILES][:, cols], op=ALU.subtract
            )

        def weigh(engine, i, cols):
            engine.tensor_tensor(out=y[i][:, cols], in0=diff[i][:, cols], in1=w_rows[i // TILES][:, cols], op=ALU.mult)

        def store_y(i, cols):
            g, j = divmod(i, TILES)
            nc.sync.dma_start(out=out_0[g, j * P : (j + 1) * P, cols], in_=y[i][:, cols])

        def weigh_on_gpsimd(i):
            weigh(nc.gpsimd, i, slice(0, GPSIMD_COLS))

        def weigh_rest_and_store(i):
            weigh(nc.vector, i, slice(GPSIMD_COLS, NP))
            store_y(i, slice(0, NP))

        def round_y(i, copy, first=0, last=NP // 16):
            if first == 0:
                y_sorted[i] = work.tile([P, NP], BF16, name="y_sorted")
            copy(
                out=y_sorted[i][:].rearrange("r (u s n e) -> r s u n e", u=2, n=4, e=2)[:, first:last],
                in_=y[i][:].rearrange("r (s n u e) -> r s u n e", n=4, u=2, e=2)[:, first:last],
            )

        def turn_y(i, tag="y_turned"):
            y_turned[i] = bank(tag)
            words = y_sorted[i][:].bitcast(F32)
            for run in range(4):
                cols = slice(run * P, (run + 1) * P)
                nc.tensor.transpose(y_turned[i][:, cols], words[:, cols], ident[:])

        def batch_units(batch):
            return range(max(2 * batch - 1, 0), min(2 * batch + 1, UNITS))

        def interleave_y(i, copy):
            batch = (i + 1) // 2
            place = i - batch_units(batch).start
            if place == 0:
                y_bf[batch] = work.tile([P, 2, 2 * 4 * P], BF16, name="y_bf", bufs=3, align_bytes=64)
            words = y_bf[batch][:].bitcast(F32)[:, :, place * 2 * P : (place + 1) * 2 * P]
            copy(
                out=words.rearrange("p c (r u) -> p c r u", u=2),
                in_=y_turned[i][:].rearrange("p (u c r) -> p c r u", u=2, c=2),
            )

        y_words = keep.tile([P, 2, G * R], U32, name="y_words", align_bytes=64)
        y_sc = keep.tile([P, 2, G * R], U8, name="y_sc", align_bytes=64)

        def quantize_y(batch, c):
            units = batch_units(batch)
            cols = slice(units.start * P, units.stop * P)
            nc.vector.quantize_mx(
                out=y_words[:, c, cols].bitcast(FP8X4),
                scales=y_sc[:, c, cols],
                in_=y_bf[batch][:, c, 0 : len(units) * 4 * P],
            )

        words_out = out_1.rearrange("c p m t -> p c (m t)").bitcast(I32)

        def store_words(batch):
            units = batch_units(batch)
            cols = slice(units.start * P, units.stop * P)
            nc.sync.dma_start(out=words_out[:, :, cols], in_=y_words[:, :, cols].bitcast(I32))

        def store_scales(first, last, queues):
            cols = slice(first * P, last * P)
            for q in range(4):
                queues[q % len(queues)].dma_start(
                    out=out_2[:, 4 * q : 4 * q + 4, cols].rearrange("c r m -> r c m").bitcast(I32),
                    in_=y_sc[32 * q : 32 * q + 4, :, cols].bitcast(I32),
                )

        quantize_x(0, x_first[:], bank("y_turned"), nc.vector.tensor_copy)
        for j in range(1, TILES):
            quantize_x(j, x_rest[:, j - 1, :], bank("pred"), nc.scalar.copy)
        gain_matmuls(0)
        round_u(0)
        gain_matmuls(1, "pred")
        round_u(1)
        turn_limits()
        turn_u(0)
        gain_matmuls(2)
        turn_u(1, "y_turned")
        apply_upper(0)
        apply_upper(1)
        apply_lower(0)
        apply_lower(1)
        quantize_u(0)
        round_u(2)
        turn_u(2)
        gain_matmuls(3)
        round_u(3)
        response_matmuls(0, 0)
        response_matmuls(0, 1)
        apply_upper(2)
        quantize_u(1)
        apply_lower(2)

        for s in range(UNITS - LEAD):
            turn_u(s + LEAD)
            if s >= 2:
                turn_y(s - 2)
            subtract_ref(s, 0)
            if s == 0:
                quantize_u(LEAD - 1)
            weigh_on_gpsimd(s)
            if s >= 1:
                round_y(s - 1, nc.scalar.copy)
            if s + LEAD + 1 < UNITS:
                gain_matmuls(s + LEAD + 1)
            apply_upper(s + LEAD)
            subtract_ref(s, 1)
            apply_lower(s + LEAD)
            weigh_rest_and_store(s)
            response_matmuls(s + 1, 0)
            response_matmuls(s + 1, 1)
            if s >= 2:
                interleave_y(s - 2, nc.scalar.copy)
            if s + LEAD + 1 < UNITS:
                round_u(s + LEAD + 1)
            if s >= 2:
                batch, c = divmod(s - 2, 2)
                quantize_y(batch, c)
                if c == 1:
                    store_words(batch)
            quantize_u(s + LEAD)
            if s in (0, TILES):
                g = s // TILES + 2
                load_gain(g)
                load_forced(g)
                load_free(g)
                load_w(g)

        a, b, z = UNITS - 3, UNITS - 2, UNITS - 1
        last_batch = UNITS // 2
        quantize_y(last_batch - 3, 1)
        store_words(last_batch - 3)
        early_units = batch_units(last_batch - 3).stop
        store_scales(0, early_units, [nc.sync])
        subtract_ref(a, 0)
        weigh_on_gpsimd(a)
        round_y(a - 1, nc.scalar.copy)
        turn_y(a - 2)
        interleave_y(a - 2, nc.scalar.copy)
        response_matmuls(b, 0)
        subtract_ref(a, 1)
        response_matmuls(b, 1)
        subtract_ref(b, 0)
        turn_y(a - 1)
        interleave_y(a - 1, nc.scalar.copy)
        response_matmuls(z, 0)
        weigh_rest_and_store(a)
        weigh_on_gpsimd(b)
        round_y(a, nc.scalar.copy)
        subtract_ref(b, 1)
        response_matmuls(z, 1)
        subtract_ref(z, 0)
        turn_y(a)
        weigh_rest_and_store(b)
        round_y(b, nc.scalar.copy)
        interleave_y(a, nc.scalar.copy)
        subtract_ref(z, 1)
        for c in range(2):
            weigh(nc.vector, z, slice(c * HALF, (c + 1) * HALF))
            store_y(z, slice(c * HALF, (c + 1) * HALF))
        for c in range(2):
            round_y(z, nc.vector.tensor_copy, c * HALF // 16, (c + 1) * HALF // 16)
        turn_y(b, "u_turned")
        interleave_y(b, nc.scalar.copy)
        for c in range(2):
            quantize_y(last_batch - 2, c)
        store_words(last_batch - 2)
        turn_y(z, "u_sums")
        interleave_y(z, nc.vector.tensor_copy)
        for c in range(2):
            quantize_y(last_batch - 1, c)
        store_words(last_batch - 1)
        for c in range(2):
            quantize_y(last_batch, c)
        store_words(last_batch)
        store_scales(early_units, UNITS, [nc.scalar, nc.sync])
